import numpy as np
import ml_dtypes


def mxq(x, axis, fmt="e4m3"):
    dtype, down = {"e4m3": (ml_dtypes.float8_e4m3fn, 7), "e5m2": (ml_dtypes.float8_e5m2, 14)}[fmt]
    v = np.moveaxis(np.asarray(x, np.float32).astype(ml_dtypes.bfloat16).astype(np.float64), axis, -1)
    blocks = v.reshape(v.shape[:-1] + (-1, 32))
    amax = np.abs(blocks).max(-1, keepdims=True)
    byte = np.maximum(np.where(amax > 0, np.frexp(amax)[1] - 1 + 127, 0) - down, 1)
    scale = np.exp2(byte - 127.0)
    codes = (blocks / scale).astype(np.float32).astype(dtype).astype(np.float64)
    return np.moveaxis((codes * scale).reshape(v.shape), -1, axis)


WIDE = False


def mx_kscale(k):
    if not WIDE:
        return np.ones(k)
    levels = np.array([30, -30])
    if k % 512:
        return np.exp2(np.random.permutation(np.resize(levels, k // 32))).repeat(32)
    a = np.empty((k // 512, 16))
    for p in range(k // 512):
        a[p, :8] = np.random.permutation(np.resize(levels, 8))
        for g in range(8):
            far = levels[np.abs(levels - a[p, g]) >= 10]
            a[p, g + 8] = far[np.random.randint(len(far))]
    return np.exp2(a.ravel()).repeat(32)


def f64(x):
    return np.asarray(x).astype(np.float64)


def striped(idx):
    return np.tile(np.asarray(idx).reshape(-1, 16).T, (8, 1)).astype(np.uint16)


def unstriped(offs):
    return offs[:16].T.reshape(-1).astype(np.int64)


E2M1 = np.array([0.0, 0.5, 1.0, 1.5, 2.0, 3.0, 4.0, 6.0, -0.0, -0.5, -1.0, -1.5, -2.0, -3.0, -4.0, -6.0])


def pack_weight(w, fmt):
    k, n = w.shape
    w = f64(np.asarray(w, np.float32).astype(ml_dtypes.bfloat16)).reshape(k // 32, 32, n)
    amax = np.abs(w).max(1)
    if fmt == "e4m3":
        byte = np.frexp(amax)[1] - 1 + 127 - 7
    else:
        mant, ex = np.frexp(amax / 6.0)
        byte = np.where(mant > 0.5, ex, ex - 1) + 127
    byte = np.clip(np.where(amax > 0, byte, 1), 1, 254)
    scaled = (w * np.exp2(127.0 - byte)[:, None, :]).reshape(k, n).astype(np.float32)
    by_word = np.ascontiguousarray(scaled.reshape(k // 512, 128, 4, n).transpose(0, 1, 3, 2))
    if fmt == "e4m3":
        words = by_word.astype(ml_dtypes.float8_e4m3fn).view(np.uint8)
    else:
        c = by_word.astype(ml_dtypes.float4_e2m1fn).view(np.uint8) & 0xF
        words = (c[..., 0::2] | (c[..., 1::2] << 4)).reshape(k // 512, 128, 2 * n)
    return np.ascontiguousarray(words), np.ascontiguousarray(byte.astype(np.uint8).reshape(k // 512, 16, n))


def unpack_weight(words, scales, fmt):
    g, _, n = scales.shape
    words = np.ascontiguousarray(words).reshape(g, 128, n, -1)
    if fmt == "e4m3":
        vals = words.view(ml_dtypes.float8_e4m3fn).astype(np.float64)
    else:
        nib = np.empty((g, 128, n, 4), np.uint8)
        nib[..., 0::2] = words & 0xF
        nib[..., 1::2] = words >> 4
        vals = E2M1[nib]
    vals = vals * np.repeat(np.exp2(scales.astype(np.float64) - 127.0), 8, axis=1)[..., None]
    return vals.transpose(0, 1, 3, 2).reshape(g * 512, n)


K, J, N, R, T, V, Q = 512, 512, 256, 256, 1024, 1024, 64


def setup_inputs():
    n = np.random.standard_normal
    idx = np.random.permutation(T)[:J]
    idx2 = np.random.permutation(V)[:J]
    fj = mx_kscale(J)
    fk = mx_kscale(K)
    drp = pack_weight(n((K, R)) * 1 / np.sqrt(K) / fk[:, None], "e2m1")
    return {
        "xf": (n((K, T))).astype(np.float32),
        "ra": (np.random.uniform(0.5, 1.5, (1, J)) * fj).astype(np.float32),
        "lo": (np.random.uniform(-0.3, 0.5, (K, 1))).astype(np.float32),
        "gt": (n((N, V)) * np.exp(0.5 * n((1, V)))).astype(np.float32),
        "rb": (np.random.uniform(0.5, 1.5, (1, J)) / fj).astype(np.float32),
        "cp": (np.random.uniform(0.4, 1.2, (N, 1))).astype(np.float32),
        "fkr": (np.random.uniform(0.5, 1.5, (1, K)) * fk).astype(np.float32),
        "dr_words": drp[0],
        "dr_scales": drp[1],
        "gr1c": (np.random.uniform(0.5, 2.0, (R, 1))).astype(np.float32),
        "offs": striped(idx),
        "offs2": striped(idx2),
    }


def reference(xf, ra, lo, gt, rb, cp, fkr, dr_words, dr_scales, gr1c, offs, offs2):
    idx = unstriped(offs)
    idx2 = unstriped(offs2)
    dru = unpack_weight(dr_words, dr_scales, "e2m1")
    us = np.maximum(f64(xf)[:, idx] - f64(lo), 0.0) * f64(ra)
    ut = us.T
    uj = ut * f64(fkr)
    gs = np.minimum(f64(gt)[:, idx2], f64(cp)) * f64(rb)
    gj = gs.T
    ujq = mxq(uj, 0, "e4m3")
    gjq = mxq(gj, 0, "e5m2")
    w = ujq.T @ gjq
    wq = mxq(w, 0, "e5m2")
    v2 = dru.T @ wq
    wq = v2.reshape(R, Q, N // Q).sum(axis=2)
    y = 0.02 * wq * f64(gr1c)
    return y

@@ -1,0 +1,199 @@
+from contextlib import ExitStack
+
+import concourse.mybir as mybir
+from concourse.masks import make_identity
+
+K, J, N, R, T, V, Q = 512, 512, 256, 256, 1024, 1024, 64
+FLOPS = 2 * J * K * N + 2 * K * R * N
+
+F32 = mybir.dt.float32
+BF16 = mybir.dt.bfloat16
+I32 = mybir.dt.int32
+U32 = mybir.dt.uint32
+U16 = mybir.dt.uint16
+U8 = mybir.dt.uint8
+E4M3 = mybir.dt.float8_e4m3fn_x4
+E5M2 = mybir.dt.float8_e5m2_x4
+E2M1 = mybir.dt.float4_e2m1fn_x4
+ALU = mybir.AluOpType
+COPY = mybir.ActivationFunctionType.Copy
+
+P = 128
+VECTOR_SHARE_G = (256, 192)
+VECTOR_SHARE_X = (192, 128, 128, 128)
+
+
+def tile_list_directions_over_bounded_sums_kernel(
+    tc, xf, ra, lo, gt, rb, cp, fkr, dr_words, dr_scales, gr1c, offs, offs2, out
+):
+    nc = tc.nc
+    with ExitStack() as ctx:
+        keep = ctx.enter_context(tc.tile_pool(name="keep", bufs=1))
+        work = ctx.enter_context(tc.tile_pool(name="work", bufs=3))
+        psum = ctx.enter_context(tc.psum_pool(name="psum", bufs=1))
+        turn = ctx.enter_context(tc.psum_pool(name="turn", bufs=3))
+
+        x_rows = xf.rearrange("(p t) c -> t p c", t=4)
+        g_rows = gt.rearrange("(p h) c -> h p c", h=2)
+
+        list_g = keep.tile([P, J // 16], U16, name="list_g")
+        list_x = keep.tile([P, J // 16], U16, name="list_x")
+        x_tab = [keep.tile([P, T], F32, name="x_tab%d" % t) for t in range(4)]
+        g_tab = [keep.tile([P, V], F32, name="g_tab%d" % h) for h in range(2)]
+        ra_t = keep.tile([P, 4], F32, name="ra_t")
+        rb_t = keep.tile([P, 4], F32, name="rb_t")
+        lo_t = keep.tile([P, 4], F32, name="lo_t")
+        fk_t = keep.tile([P, 4], F32, name="fk_t")
+        cp_t = keep.tile([P, 2], F32, name="cp_t")
+        gr_t = keep.tile([P, 2, 1], F32, name="gr_t")
+        d_words = keep.tile([P, 2 * R], U8, name="d_words", align_bytes=64)
+        d_scales = keep.tile([P, R], U8, name="d_scales", align_bytes=64)
+        ident = keep.tile([P, P], F32, name="ident")
+
+        make_identity(nc, ident[:])
+        nc.gpsimd.memset(d_scales[:].bitcast(I32), 0)
+
+        nc.sync.dma_start(list_g[:], offs2)
+        nc.scalar.dma_start(rb_t[:], rb[0].rearrange("(p t) -> p t", t=4))
+        nc.sync.dma_start(g_tab[0][:], g_rows[0])
+        nc.scalar.dma_start(cp_t[:], cp.rearrange("(p h) o -> p (h o)", h=2))
+        nc.sync.dma_start(list_x[:], offs)
+        nc.scalar.dma_start(ra_t[:], ra[0].rearrange("(p t) -> p t", t=4))
+        nc.sync.dma_start(x_tab[0][:], x_rows[0])
+        nc.scalar.dma_start(lo_t[:], lo.rearrange("(p t) o -> p (t o)", t=4))
+        nc.scalar.dma_start(fk_t[:], fkr[0].rearrange("(p t) -> p t", t=4))
+        for t in range(1, 4):
+            nc.sync.dma_start(x_tab[t][:], x_rows[t])
+        nc.sync.dma_start(g_tab[1][:], g_rows[1])
+        nc.sync.dma_start(d_words[:], dr_words[0])
+        for quad in range(4):
+            nc.sync.dma_start(
+                d_scales[32 * quad : 32 * quad + 4, :].bitcast(I32),
+                dr_scales[0, 4 * quad : 4 * quad + 4, :].bitcast(I32),
+            )
+        with nc.allow_non_contiguous_dma(reason="one factor a partition"):
+            nc.sync.dma_start(gr_t[:], gr1c.rearrange("(h p) o -> p h o", h=2))
+
+        def spread(vec, tag):
+            bank = psum.tile([P, J], F32, name=tag, tag=tag)
+            by_t = bank[:].rearrange("p (u b m t) -> p t b u m", u=2, b=16, m=4, t=4)
+            for t in range(4):
+                nc.tensor.transpose(by_t[:, t], vec[:, t : t + 1].to_broadcast([P, P]), ident[:])
+            return bank
+
+        def gather(table, offsets, share):
+            picked = work.tile([P, J], F32, name="picked")
+            nc.vector.tensor_copy(picked[:, :share], table[:].indirect(offsets[:, : share // 16]))
+            nc.scalar.activation(picked[:, share:], table[:].indirect(offsets[:, share // 16 :]), COPY)
+            return picked[:].rearrange("p (b u s) -> p u b s", u=2, s=16)
+
+        def turn_and_quantize(rounded, fmt, name):
+            words = rounded[:].bitcast(F32)
+            bank = turn.tile([P, 2, P], F32, name="turned")
+            for u in range(2):
+                nc.tensor.transpose(bank[:, u, :], words[:, P * u : P * (u + 1)], ident[:])
+            grouped = work.tile([P, 4 * P], BF16, name="grouped", align_bytes=64)
+            nc.scalar.copy(
+                grouped[:].bitcast(F32).rearrange("p (c u) -> p c u", u=2),
+                bank[:].rearrange("p u c -> p c u"),
+            )
+            codes = keep.tile([P, P], U32, name=name + "_codes", align_bytes=64)
+            scales = keep.tile([P, P], U8, name=name + "_scales", align_bytes=64)
+            nc.vector.quantize_mx(codes[:].bitcast(fmt), scales[:], grouped[:])
+            return codes, scales
+
+        def g_operand(h):
+            picked = gather(g_tab[h], list_g, VECTOR_SHARE_G[h])
+            rounded = work.tile([P, J], BF16, name="rounded", align_bytes=64)
+            rounded_v = rounded[:].rearrange("p (u b s) -> p u b s", u=2, s=16)
+            rb_v = rb_all[:].rearrange("p (u b s) -> p u b s", u=2, s=16)
+            for u in range(2):
+                nc.vector.scalar_tensor_tensor(
+                    rounded_v[:, u], picked[:, u], cp_t[:, h : h + 1], rb_v[:, u], ALU.min, ALU.mult
+                )
+            return turn_and_quantize(rounded, E5M2, "g%d" % h)
+
+        def u_operand(t):
+            picked = gather(x_tab[t], list_x, VECTOR_SHARE_X[t])
+            excess = work.tile([P, J], F32, name="excess")
+            nc.vector.tensor_scalar(
+                excess[:].rearrange("p (u b s) -> p u b s", u=2, s=16),
+                picked,
+                lo_t[:, t : t + 1],
+                0.0,
+                ALU.subtract,
+                ALU.max,
+            )
+            rounded = work.tile([P, J], BF16, name="rounded", align_bytes=64)
+            nc.vector.scalar_tensor_tensor(
+                rounded[:], excess[:], fk_t[:, t : t + 1], ra_all[:], ALU.mult, ALU.mult
+            )
+            return turn_and_quantize(rounded, E4M3, "u%d" % t)
+
+        def moment(bank, t, u_op, g_op):
+            nc.tensor.matmul_mx(
+                bank[:, t, :],
+                lhsT=u_op[0][:].bitcast(E4M3),
+                lhsT_scale=u_op[1][:],
+                rhs=g_op[0][:].bitcast(E5M2),
+                rhs_scale=g_op[1][:],
+                start=True,
+                stop=True,
+            )
+
+        def directions(h, w_bank, v_banks):
+            w_grouped = keep.tile([P, P, 4], BF16, name="w_grouped%d" % h, align_bytes=64)
+            w_view = w_bank[:].rearrange("p t n -> p n t")
+            if h == 0:
+                nc.scalar.copy(w_grouped[:], w_view)
+            else:
+                nc.vector.tensor_copy(w_grouped[:], w_view)
+            codes = keep.tile([P, P], U32, name="w_codes%d" % h, align_bytes=64)
+            scales = keep.tile([P, P], U8, name="w_scales%d" % h, align_bytes=64)
+            nc.vector.quantize_mx(
+                codes[:].bitcast(E5M2), scales[:], w_grouped[:].rearrange("p n t -> p (n t)")
+            )
+            for half in range(2):
+                nc.tensor.matmul_mx(
+                    v_banks[half][:],
+                    lhsT=d_words[:, 2 * P * half : 2 * P * (half + 1)].bitcast(E2M1),
+                    lhsT_scale=d_scales[:, P * half : P * (half + 1)],
+                    rhs=codes[:].bitcast(E5M2),
+                    rhs_scale=scales[:],
+                    start=(h == 0),
+                    stop=(h == 1),
+                )
+
+        rb_all = spread(rb_t, "rb_all")
+        ra_all = spread(ra_t, "ra_all")
+        w_banks = [psum.tile([P, 4, P], F32, name="w_bank%d" % h) for h in range(2)]
+
+        g0 = g_operand(0)
+        u_ops = []
+        for t in range(4):
+            u_ops.append(u_operand(t))
+            moment(w_banks[0], t, u_ops[t], g0)
+        g1 = g_operand(1)
+        v_banks = [
+            psum.tile([P, P], F32, name="v_bank0", tag="ra_all"),
+            psum.tile([P, P], F32, name="v_bank1"),
+        ]
+        directions(0, w_banks[0], v_banks)
+        for t in range(4):
+            moment(w_banks[1], t, u_ops[t], g1)
+        directions(1, w_banks[1], v_banks)
+
+        summed = keep.tile([P, 2, Q], F32, name="summed")
+        result = keep.tile([P, 2, Q], F32, name="result")
+        for half in range(2):
+            nc.vector.tensor_reduce(
+                summed[:, half, :],
+                v_banks[half][:].rearrange("p (q e) -> p q e", e=2),
+                mybir.AxisListType.X,
+                ALU.add,
+            )
+        for half in range(2):
+            nc.vector.tensor_scalar(
+                result[:, half, :], summed[:, half, :], gr_t[:, half, :], 0.02, ALU.mult, ALU.mult
+            )
+        nc.sync.dma_start(out.rearrange("(h p) q -> p h q", h=2), result[:])

@@ -19,8 +19,8 @@ ALU = mybir.AluOpType
 COPY = mybir.ActivationFunctionType.Copy
 
 P = 128
-VECTOR_SHARE_G = (256, 192)
-VECTOR_SHARE_X = (192, 128, 128, 128)
+VECTOR_SHARE_G0 = 256
+VECTOR_SHARE_X0 = 192
 
 
 def tile_list_directions_over_bounded_sums_kernel(
@@ -31,39 +31,41 @@ def tile_list_directions_over_bounded_sums_kernel(
         keep = ctx.enter_context(tc.tile_pool(name="keep", bufs=1))
         work = ctx.enter_context(tc.tile_pool(name="work", bufs=3))
         psum = ctx.enter_context(tc.psum_pool(name="psum", bufs=1))
-        turn = ctx.enter_context(tc.psum_pool(name="turn", bufs=3))
 
         x_rows = xf.rearrange("(p t) c -> t p c", t=4)
         g_rows = gt.rearrange("(p h) c -> h p c", h=2)
 
         list_g = keep.tile([P, J // 16], U16, name="list_g")
         list_x = keep.tile([P, J // 16], U16, name="list_x")
-        x_tab = [keep.tile([P, T], F32, name="x_tab%d" % t) for t in range(4)]
-        g_tab = [keep.tile([P, V], F32, name="g_tab%d" % h) for h in range(2)]
+        x_tab = [keep.tile([P, T], F32, name="x_tab%d" % t, align_bytes=64) for t in range(4)]
+        g_tab = [keep.tile([P, V], F32, name="g_tab%d" % h, align_bytes=64) for h in range(2)]
         ra_t = keep.tile([P, 4], F32, name="ra_t")
-        rb_t = keep.tile([P, 4], F32, name="rb_t")
+        rb_t = keep.tile([P, 4], F32, name="rb_t", tag="chain_b", align_bytes=64)
         lo_t = keep.tile([P, 4], F32, name="lo_t")
         fk_t = keep.tile([P, 4], F32, name="fk_t")
-        cp_t = keep.tile([P, 2], F32, name="cp_t")
+        cp_t = keep.tile([P, 2], F32, name="cp_t", align_bytes=64)
         gr_t = keep.tile([P, 2, 1], F32, name="gr_t")
         d_words = keep.tile([P, 2 * R], U8, name="d_words", align_bytes=64)
         d_scales = keep.tile([P, R], U8, name="d_scales", align_bytes=64)
         ident = keep.tile([P, P], F32, name="ident")
 
-        make_identity(nc, ident[:])
+        ident_bf16 = keep.tile([P, P], BF16, name="ident_bf16", tag="chain_a", align_bytes=64)
+        make_identity(nc, ident_bf16[:])
+        nc.scalar.activation(ident[:], ident_bf16[:], COPY)
         nc.gpsimd.memset(d_scales[:].bitcast(I32), 0)
 
+        nc.sync.dma_start(rb_t[:], rb[0].rearrange("(p t) -> p t", t=4))
+        nc.sync.dma_start(ra_t[:], ra[0].rearrange("(p t) -> p t", t=4))
         nc.sync.dma_start(list_g[:], offs2)
-        nc.scalar.dma_start(rb_t[:], rb[0].rearrange("(p t) -> p t", t=4))
+        nc.sync.dma_start(cp_t[:], cp.rearrange("(p h) o -> p (h o)", h=2))
         nc.sync.dma_start(g_tab[0][:], g_rows[0])
-        nc.scalar.dma_start(cp_t[:], cp.rearrange("(p h) o -> p (h o)", h=2))
         nc.sync.dma_start(list_x[:], offs)
-        nc.scalar.dma_start(ra_t[:], ra[0].rearrange("(p t) -> p t", t=4))
+        nc.sync.dma_start(lo_t[:], lo.rearrange("(p t) o -> p (t o)", t=4))
         nc.sync.dma_start(x_tab[0][:], x_rows[0])
-        nc.scalar.dma_start(lo_t[:], lo.rearrange("(p t) o -> p (t o)", t=4))
-        nc.scalar.dma_start(fk_t[:], fkr[0].rearrange("(p t) -> p t", t=4))
-        for t in range(1, 4):
-            nc.sync.dma_start(x_tab[t][:], x_rows[t])
+        nc.sync.dma_start(fk_t[:], fkr[0].rearrange("(p t) -> p t", t=4))
+        nc.sync.dma_start(x_tab[1][:], x_rows[1])
+        nc.sync.dma_start(x_tab[2][:], x_rows[2])
+        nc.sync.dma_start(x_tab[3][:], x_rows[3])
         nc.sync.dma_start(g_tab[1][:], g_rows[1])
         nc.sync.dma_start(d_words[:], dr_words[0])
         for quad in range(4):
@@ -81,41 +83,41 @@ def tile_list_directions_over_bounded_sums_kernel(
                 nc.tensor.transpose(by_t[:, t], vec[:, t : t + 1].to_broadcast([P, P]), ident[:])
             return bank
 
-        def gather(table, offsets, share):
-            picked = work.tile([P, J], F32, name="picked")
-            nc.vector.tensor_copy(picked[:, :share], table[:].indirect(offsets[:, : share // 16]))
+        def gather(table, offsets, share, tag):
+            picked = keep.tile([P, J], F32, name="picked", tag=tag, align_bytes=64)
+            if share:
+                nc.vector.tensor_copy(picked[:, :share], table[:].indirect(offsets[:, : share // 16]))
             nc.scalar.activation(picked[:, share:], table[:].indirect(offsets[:, share // 16 :]), COPY)
             return picked[:].rearrange("p (b u s) -> p u b s", u=2, s=16)
 
-        def turn_and_quantize(rounded, fmt, name):
+        def turn_pairs(rounded, bank):
             words = rounded[:].bitcast(F32)
-            bank = turn.tile([P, 2, P], F32, name="turned")
             for u in range(2):
                 nc.tensor.transpose(bank[:, u, :], words[:, P * u : P * (u + 1)], ident[:])
-            grouped = work.tile([P, 4 * P], BF16, name="grouped", align_bytes=64)
-            nc.scalar.copy(
-                grouped[:].bitcast(F32).rearrange("p (c u) -> p c u", u=2),
-                bank[:].rearrange("p u c -> p c u"),
-            )
-            codes = keep.tile([P, P], U32, name=name + "_codes", align_bytes=64)
-            scales = keep.tile([P, P], U8, name=name + "_scales", align_bytes=64)
-            nc.vector.quantize_mx(codes[:].bitcast(fmt), scales[:], grouped[:])
-            return codes, scales
 
-        def g_operand(h):
-            picked = gather(g_tab[h], list_g, VECTOR_SHARE_G[h])
-            rounded = work.tile([P, J], BF16, name="rounded", align_bytes=64)
+        def quantize(bank, tiles, fmt, name, copy, grouped_tag, codes_tag):
+            grouped = keep.tile([P, tiles * 4 * P], BF16, name=name + "_grouped", tag=grouped_tag, align_bytes=64)
+            copy(
+                grouped[:].bitcast(F32).rearrange("p (a c u) -> p a c u", a=tiles, u=2),
+                bank[:].rearrange("p a u c -> p a c u"),
+            )
+            codes = keep.tile([P, tiles * P], U32, name=name + "_codes", tag=codes_tag, align_bytes=64)
+            scales = keep.tile([P, tiles * P], U8, name=name + "_scales", align_bytes=64)
+            nc.vector.quantize_mx(codes[:].bitcast(fmt), scales[:], grouped[:])
+            return [(codes[:, P * a : P * (a + 1)], scales[:, P * a : P * (a + 1)]) for a in range(tiles)]
+
+        def g_values(h, picked, bank, tag):
+            rounded = keep.tile([P, J], BF16, name="rounded_g", tag=tag, align_bytes=64)
             rounded_v = rounded[:].rearrange("p (u b s) -> p u b s", u=2, s=16)
             rb_v = rb_all[:].rearrange("p (u b s) -> p u b s", u=2, s=16)
             for u in range(2):
                 nc.vector.scalar_tensor_tensor(
                     rounded_v[:, u], picked[:, u], cp_t[:, h : h + 1], rb_v[:, u], ALU.min, ALU.mult
                 )
-            return turn_and_quantize(rounded, E5M2, "g%d" % h)
+            turn_pairs(rounded, bank)
 
-        def u_operand(t):
-            picked = gather(x_tab[t], list_x, VECTOR_SHARE_X[t])
-            excess = work.tile([P, J], F32, name="excess")
+        def u_values(t, picked, bank):
+            excess = keep.tile([P, J], F32, name="excess", tag="excess", align_bytes=64)
             nc.vector.tensor_scalar(
                 excess[:].rearrange("p (u b s) -> p u b s", u=2, s=16),
                 picked,
@@ -128,15 +130,15 @@ def tile_list_directions_over_bounded_sums_kernel(
             nc.vector.scalar_tensor_tensor(
                 rounded[:], excess[:], fk_t[:, t : t + 1], ra_all[:], ALU.mult, ALU.mult
             )
-            return turn_and_quantize(rounded, E4M3, "u%d" % t)
+            turn_pairs(rounded, bank)
 
         def moment(bank, t, u_op, g_op):
             nc.tensor.matmul_mx(
                 bank[:, t, :],
-                lhsT=u_op[0][:].bitcast(E4M3),
-                lhsT_scale=u_op[1][:],
-                rhs=g_op[0][:].bitcast(E5M2),
-                rhs_scale=g_op[1][:],
+                lhsT=u_op[0].bitcast(E4M3),
+                lhsT_scale=u_op[1],
+                rhs=g_op[0].bitcast(E5M2),
+                rhs_scale=g_op[1],
                 start=True,
                 stop=True,
             )
@@ -144,10 +146,7 @@ def tile_list_directions_over_bounded_sums_kernel(
         def directions(h, w_bank, v_banks):
             w_grouped = keep.tile([P, P, 4], BF16, name="w_grouped%d" % h, align_bytes=64)
             w_view = w_bank[:].rearrange("p t n -> p n t")
-            if h == 0:
-                nc.scalar.copy(w_grouped[:], w_view)
-            else:
-                nc.vector.tensor_copy(w_grouped[:], w_view)
+            nc.scalar.copy(w_grouped[:], w_view)
             codes = keep.tile([P, P], U32, name="w_codes%d" % h, align_bytes=64)
             scales = keep.tile([P, P], U8, name="w_scales%d" % h, align_bytes=64)
             nc.vector.quantize_mx(
@@ -168,19 +167,29 @@ def tile_list_directions_over_bounded_sums_kernel(
         ra_all = spread(ra_t, "ra_all")
         w_banks = [psum.tile([P, 4, P], F32, name="w_bank%d" % h) for h in range(2)]
 
-        g0 = g_operand(0)
-        u_ops = []
+        g_bank = psum.tile([P, 1, 2, P], F32, name="g_bank")
+        u_banks = [psum.tile([P, 2, 2, P], F32, name="u_bank%d" % a) for a in range(2)]
+
+        g_values(0, gather(g_tab[0], list_g, VECTOR_SHARE_G0, "chain_a"), g_bank[:, 0], "rounded_g0")
+        u_values(0, gather(x_tab[0], list_x, VECTOR_SHARE_X0, "chain_b"), u_banks[0][:, 0])
+        (g0,) = quantize(g_bank, 1, E5M2, "g0", nc.vector.tensor_copy, "g0_grouped", "g0_codes")
+        u_values(1, gather(x_tab[1], list_x, 0, "chain_a"), u_banks[0][:, 1])
+        u_values(2, gather(x_tab[2], list_x, 0, "chain_b"), u_banks[1][:, 0])
+        u_values(3, gather(x_tab[3], list_x, 0, "chain_a"), u_banks[1][:, 1])
+        g_bank = psum.tile([P, 1, 2, P], F32, name="g_bank")
+        g_values(1, gather(g_tab[1], list_g, 0, "chain_b"), g_bank[:, 0], "excess")
+        u_ops = quantize(u_banks[0], 2, E4M3, "u01", nc.scalar.copy, "g_tab1", "chain_b")
+        u_ops = u_ops + quantize(u_banks[1], 2, E4M3, "u23", nc.scalar.copy, "u23_grouped", "cp_t")
+        (g1,) = quantize(g_bank, 1, E5M2, "g1", nc.scalar.copy, "g1_grouped", "g1_codes")
         for t in range(4):
-            u_ops.append(u_operand(t))
             moment(w_banks[0], t, u_ops[t], g0)
-        g1 = g_operand(1)
+        for t in range(4):
+            moment(w_banks[1], t, u_ops[t], g1)
         v_banks = [
             psum.tile([P, P], F32, name="v_bank0", tag="ra_all"),
             psum.tile([P, P], F32, name="v_bank1"),
         ]
         directions(0, w_banks[0], v_banks)
-        for t in range(4):
-            moment(w_banks[1], t, u_ops[t], g1)
         directions(1, w_banks[1], v_banks)
 
         summed = keep.tile([P, 2, Q], F32, name="summed")

@@ -19,6 +19,7 @@ ALU = mybir.AluOpType
 COPY = mybir.ActivationFunctionType.Copy
 
 P = 128
+HALF = J // 2
 VECTOR_SHARE_G0 = 256
 VECTOR_SHARE_X0 = 192
 
@@ -54,11 +55,11 @@ def tile_list_directions_over_bounded_sums_kernel(
         nc.scalar.activation(ident[:], ident_bf16[:], COPY)
         nc.gpsimd.memset(d_scales[:].bitcast(I32), 0)
 
-        nc.sync.dma_start(rb_t[:], rb[0].rearrange("(p t) -> p t", t=4))
-        nc.sync.dma_start(ra_t[:], ra[0].rearrange("(p t) -> p t", t=4))
+        nc.scalar.dma_start(rb_t[:], rb[0].rearrange("(p t) -> p t", t=4))
         nc.sync.dma_start(list_g[:], offs2)
-        nc.sync.dma_start(cp_t[:], cp.rearrange("(p h) o -> p (h o)", h=2))
         nc.sync.dma_start(g_tab[0][:], g_rows[0])
+        nc.sync.dma_start(cp_t[:], cp.rearrange("(p h) o -> p (h o)", h=2))
+        nc.sync.dma_start(ra_t[:], ra[0].rearrange("(p t) -> p t", t=4))
         nc.sync.dma_start(list_x[:], offs)
         nc.sync.dma_start(lo_t[:], lo.rearrange("(p t) o -> p (t o)", t=4))
         nc.sync.dma_start(x_tab[0][:], x_rows[0])
@@ -90,10 +91,8 @@ def tile_list_directions_over_bounded_sums_kernel(
             nc.scalar.activation(picked[:, share:], table[:].indirect(offsets[:, share // 16 :]), COPY)
             return picked[:].rearrange("p (b u s) -> p u b s", u=2, s=16)
 
-        def turn_pairs(rounded, bank):
-            words = rounded[:].bitcast(F32)
-            for u in range(2):
-                nc.tensor.transpose(bank[:, u, :], words[:, P * u : P * (u + 1)], ident[:])
+        def turn_pairs(rounded, out_half):
+            nc.tensor.transpose(out_half, rounded[:].bitcast(F32), ident[:])
 
         def quantize(bank, tiles, fmt, name, copy, grouped_tag, codes_tag):
             grouped = keep.tile([P, tiles * 4 * P], BF16, name=name + "_grouped", tag=grouped_tag, align_bytes=64)
@@ -107,30 +106,41 @@ def tile_list_directions_over_bounded_sums_kernel(
             return [(codes[:, P * a : P * (a + 1)], scales[:, P * a : P * (a + 1)]) for a in range(tiles)]
 
         def g_values(h, picked, bank, tag):
-            rounded = keep.tile([P, J], BF16, name="rounded_g", tag=tag, align_bytes=64)
-            rounded_v = rounded[:].rearrange("p (u b s) -> p u b s", u=2, s=16)
-            rb_v = rb_all[:].rearrange("p (u b s) -> p u b s", u=2, s=16)
             for u in range(2):
+                rounded = keep.tile([P, HALF], BF16, name="rounded_g", tag="%s%d" % (tag, u), align_bytes=64)
                 nc.vector.scalar_tensor_tensor(
-                    rounded_v[:, u], picked[:, u], cp_t[:, h : h + 1], rb_v[:, u], ALU.min, ALU.mult
+                    rounded[:].rearrange("p (b s) -> p b s", s=16),
+                    picked[:, u],
+                    cp_t[:, h : h + 1],
+                    rb_all[:, HALF * u : HALF * (u + 1)].rearrange("p (b s) -> p b s", s=16),
+                    ALU.min,
+                    ALU.mult,
                 )
-            turn_pairs(rounded, bank)
+                turn_pairs(rounded, bank[:, u, :])
 
         def u_values(t, picked, bank):
-            excess = keep.tile([P, J], F32, name="excess", tag="excess", align_bytes=64)
-            nc.vector.tensor_scalar(
-                excess[:].rearrange("p (u b s) -> p u b s", u=2, s=16),
-                picked,
-                lo_t[:, t : t + 1],
-                0.0,
-                ALU.subtract,
-                ALU.max,
-            )
-            rounded = work.tile([P, J], BF16, name="rounded", align_bytes=64)
-            nc.vector.scalar_tensor_tensor(
-                rounded[:], excess[:], fk_t[:, t : t + 1], ra_all[:], ALU.mult, ALU.mult
-            )
-            turn_pairs(rounded, bank)
+            excess = []
+            for u in range(2):
+                excess.append(keep.tile([P, HALF], F32, name="excess", tag="excess%d" % u, align_bytes=64))
+                nc.vector.tensor_scalar(
+                    excess[u][:].rearrange("p (b s) -> p b s", s=16),
+                    picked[:, u],
+                    lo_t[:, t : t + 1],
+                    0.0,
+                    ALU.subtract,
+                    ALU.max,
+                )
+            for u in range(2):
+                rounded = work.tile([P, HALF], BF16, name="rounded", bufs=4, align_bytes=64)
+                nc.vector.scalar_tensor_tensor(
+                    rounded[:],
+                    excess[u][:],
+                    fk_t[:, t : t + 1],
+                    ra_all[:, HALF * u : HALF * (u + 1)],
+                    ALU.mult,
+                    ALU.mult,
+                )
+                turn_pairs(rounded, bank[:, u, :])
 
         def moment(bank, t, u_op, g_op):
             nc.tensor.matmul_mx(
@@ -167,20 +177,23 @@ def tile_list_directions_over_bounded_sums_kernel(
         ra_all = spread(ra_t, "ra_all")
         w_banks = [psum.tile([P, 4, P], F32, name="w_bank%d" % h) for h in range(2)]
 
-        g_bank = psum.tile([P, 1, 2, P], F32, name="g_bank")
-        u_banks = [psum.tile([P, 2, 2, P], F32, name="u_bank%d" % a) for a in range(2)]
+        g0_bank = psum.tile([P, 1, 2, P], F32, name="g0_bank")
+        u01_bank = psum.tile([P, 2, 2, P], F32, name="u01_bank")
+        u3_bank = psum.tile([P, 1, 2, P], F32, name="u3_bank")
+        g1_bank = psum.tile([P, 1, 2, P], F32, name="g1_bank", tag="v_bank1")
 
-        g_values(0, gather(g_tab[0], list_g, VECTOR_SHARE_G0, "chain_a"), g_bank[:, 0], "rounded_g0")
-        u_values(0, gather(x_tab[0], list_x, VECTOR_SHARE_X0, "chain_b"), u_banks[0][:, 0])
-        (g0,) = quantize(g_bank, 1, E5M2, "g0", nc.vector.tensor_copy, "g0_grouped", "g0_codes")
-        u_values(1, gather(x_tab[1], list_x, 0, "chain_a"), u_banks[0][:, 1])
-        u_values(2, gather(x_tab[2], list_x, 0, "chain_b"), u_banks[1][:, 0])
-        u_values(3, gather(x_tab[3], list_x, 0, "chain_a"), u_banks[1][:, 1])
-        g_bank = psum.tile([P, 1, 2, P], F32, name="g_bank")
-        g_values(1, gather(g_tab[1], list_g, 0, "chain_b"), g_bank[:, 0], "excess")
-        u_ops = quantize(u_banks[0], 2, E4M3, "u01", nc.scalar.copy, "g_tab1", "chain_b")
-        u_ops = u_ops + quantize(u_banks[1], 2, E4M3, "u23", nc.scalar.copy, "u23_grouped", "cp_t")
-        (g1,) = quantize(g_bank, 1, E5M2, "g1", nc.scalar.copy, "g1_grouped", "g1_codes")
+        g_values(0, gather(g_tab[0], list_g, VECTOR_SHARE_G0, "chain_a"), g0_bank[:, 0], "rounded_g0")
+        u_values(0, gather(x_tab[0], list_x, VECTOR_SHARE_X0, "chain_b"), u01_bank[:, 0])
+        (g0,) = quantize(g0_bank, 1, E5M2, "g0", nc.vector.tensor_copy, "g0_grouped", "g0_codes")
+        u2_bank = psum.tile([P, 1, 2, P], F32, name="u2_bank", tag="g0_bank")
+        u_values(1, gather(x_tab[1], list_x, 0, "chain_a"), u01_bank[:, 1])
+        u_values(2, gather(x_tab[2], list_x, 0, "chain_b"), u2_bank[:, 0])
+        u_values(3, gather(x_tab[3], list_x, 0, "chain_a"), u3_bank[:, 0])
+        g_values(1, gather(g_tab[1], list_g, 0, "chain_b"), g1_bank[:, 0], "excess")
+        u_ops = quantize(u01_bank, 2, E4M3, "u01", nc.scalar.copy, "g_tab1", "chain_b")
+        u_ops = u_ops + quantize(u2_bank, 1, E4M3, "u2", nc.scalar.copy, "u2_grouped", "cp_t")
+        u_ops = u_ops + quantize(u3_bank, 1, E4M3, "u3", nc.scalar.copy, "u3_grouped", "u3_codes")
+        (g1,) = quantize(g1_bank, 1, E5M2, "g1", nc.scalar.copy, "g1_grouped", "g1_codes")
         for t in range(4):
             moment(w_banks[0], t, u_ops[t], g0)
         for t in range(4):
@@ -192,17 +205,14 @@ def tile_list_directions_over_bounded_sums_kernel(
         directions(0, w_banks[0], v_banks)
         directions(1, w_banks[1], v_banks)
 
-        summed = keep.tile([P, 2, Q], F32, name="summed")
+        factor = keep.tile([P, 2, 1], F32, name="factor")
+        nc.gpsimd.tensor_scalar(factor[:], gr_t[:], 0.02, 0.0, ALU.mult, ALU.add)
+        even = keep.tile([P, 2, Q], F32, name="even")
         result = keep.tile([P, 2, Q], F32, name="result")
         for half in range(2):
-            nc.vector.tensor_reduce(
-                summed[:, half, :],
-                v_banks[half][:].rearrange("p (q e) -> p q e", e=2),
-                mybir.AxisListType.X,
-                ALU.add,
-            )
-        for half in range(2):
-            nc.vector.tensor_scalar(
-                result[:, half, :], summed[:, half, :], gr_t[:, half, :], 0.02, ALU.mult, ALU.mult
+            pairs = v_banks[half][:].rearrange("p (q e) -> p e q", e=2)
+            nc.scalar.activation(even[:, half, :], pairs[:, 0], COPY, scale=factor[:, half, :])
+            nc.vector.scalar_tensor_tensor(
+                result[:, half, :], pairs[:, 1], factor[:, half, :], even[:, half, :], ALU.mult, ALU.add
             )
         nc.sync.dma_start(out.rearrange("(h p) q -> p h q", h=2), result[:])

from contextlib import ExitStack

import concourse.mybir as mybir
from concourse.masks import make_identity

K, J, N, R, T, V, Q = 512, 512, 256, 256, 1024, 1024, 64
FLOPS = 2 * J * K * N + 2 * K * R * N

F32 = mybir.dt.float32
BF16 = mybir.dt.bfloat16
I32 = mybir.dt.int32
U32 = mybir.dt.uint32
U16 = mybir.dt.uint16
U8 = mybir.dt.uint8
E4M3 = mybir.dt.float8_e4m3fn_x4
E5M2 = mybir.dt.float8_e5m2_x4
E2M1 = mybir.dt.float4_e2m1fn_x4
ALU = mybir.AluOpType
COPY = mybir.ActivationFunctionType.Copy

P = 128
HALF = J // 2
VECTOR_SHARE_G0 = 256
VECTOR_SHARE_X0 = 192


def tile_list_directions_over_bounded_sums_kernel(
    tc, xf, ra, lo, gt, rb, cp, fkr, dr_words, dr_scales, gr1c, offs, offs2, out
):
    nc = tc.nc
    with ExitStack() as ctx:
        keep = ctx.enter_context(tc.tile_pool(name="keep", bufs=1))
        work = ctx.enter_context(tc.tile_pool(name="work", bufs=3))
        psum = ctx.enter_context(tc.psum_pool(name="psum", bufs=1))

        x_rows = xf.rearrange("(p t) c -> t p c", t=4)
        g_rows = gt.rearrange("(p h) c -> h p c", h=2)

        list_g = keep.tile([P, J // 16], U16, name="list_g")
        list_x = keep.tile([P, J // 16], U16, name="list_x")
        x_tab = [keep.tile([P, T], F32, name="x_tab%d" % t, align_bytes=64) for t in range(4)]
        g_tab = [keep.tile([P, V], F32, name="g_tab%d" % h, align_bytes=64) for h in range(2)]
        ra_t = keep.tile([P, 4], F32, name="ra_t")
        rb_t = keep.tile([P, 4], F32, name="rb_t", tag="chain_b", align_bytes=64)
        lo_t = keep.tile([P, 4], F32, name="lo_t")
        fk_t = keep.tile([P, 4], F32, name="fk_t")
        cp_t = keep.tile([P, 2], F32, name="cp_t", align_bytes=64)
        gr_t = keep.tile([P, 2, 1], F32, name="gr_t")
        d_words = keep.tile([P, 2 * R], U8, name="d_words", align_bytes=64)
        d_scales = keep.tile([P, R], U8, name="d_scales", align_bytes=64)
        ident = keep.tile([P, P], F32, name="ident")

        ident_bf16 = keep.tile([P, P], BF16, name="ident_bf16", tag="chain_a", align_bytes=64)
        make_identity(nc, ident_bf16[:])
        nc.scalar.activation(ident[:], ident_bf16[:], COPY)
        nc.gpsimd.memset(d_scales[:].bitcast(I32), 0)

        nc.scalar.dma_start(rb_t[:], rb[0].rearrange("(p t) -> p t", t=4))
        nc.sync.dma_start(list_g[:], offs2)
        nc.sync.dma_start(g_tab[0][:], g_rows[0])
        nc.sync.dma_start(cp_t[:], cp.rearrange("(p h) o -> p (h o)", h=2))
        nc.sync.dma_start(ra_t[:], ra[0].rearrange("(p t) -> p t", t=4))
        nc.sync.dma_start(list_x[:], offs)
        nc.sync.dma_start(lo_t[:], lo.rearrange("(p t) o -> p (t o)", t=4))
        nc.sync.dma_start(x_tab[0][:], x_rows[0])
        nc.sync.dma_start(fk_t[:], fkr[0].rearrange("(p t) -> p t", t=4))
        nc.sync.dma_start(x_tab[1][:], x_rows[1])
        nc.sync.dma_start(x_tab[2][:], x_rows[2])
        nc.sync.dma_start(x_tab[3][:], x_rows[3])
        nc.sync.dma_start(g_tab[1][:], g_rows[1])
        nc.sync.dma_start(d_words[:], dr_words[0])
        for quad in range(4):
            nc.sync.dma_start(
                d_scales[32 * quad : 32 * quad + 4, :].bitcast(I32),
                dr_scales[0, 4 * quad : 4 * quad + 4, :].bitcast(I32),
            )
        with nc.allow_non_contiguous_dma(reason="one factor a partition"):
            nc.sync.dma_start(gr_t[:], gr1c.rearrange("(h p) o -> p h o", h=2))

        def spread(vec, tag):
            bank = psum.tile([P, J], F32, name=tag, tag=tag)
            by_t = bank[:].rearrange("p (u b m t) -> p t b u m", u=2, b=16, m=4, t=4)
            for t in range(4):
                nc.tensor.transpose(by_t[:, t], vec[:, t : t + 1].to_broadcast([P, P]), ident[:])
            return bank

        def gather(table, offsets, share, tag):
            picked = keep.tile([P, J], F32, name="picked", tag=tag, align_bytes=64)
            if share:
                nc.vector.tensor_copy(picked[:, :share], table[:].indirect(offsets[:, : share // 16]))
            nc.scalar.activation(picked[:, share:], table[:].indirect(offsets[:, share // 16 :]), COPY)
            return picked[:].rearrange("p (b u s) -> p u b s", u=2, s=16)

        def turn_pairs(rounded, out_half):
            nc.tensor.transpose(out_half, rounded[:].bitcast(F32), ident[:])

        def quantize(bank, tiles, fmt, name, copy, grouped_tag, codes_tag):
            grouped = keep.tile([P, tiles * 4 * P], BF16, name=name + "_grouped", tag=grouped_tag, align_bytes=64)
            copy(
                grouped[:].bitcast(F32).rearrange("p (a c u) -> p a c u", a=tiles, u=2),
                bank[:].rearrange("p a u c -> p a c u"),
            )
            codes = keep.tile([P, tiles * P], U32, name=name + "_codes", tag=codes_tag, align_bytes=64)
            scales = keep.tile([P, tiles * P], U8, name=name + "_scales", align_bytes=64)
            nc.vector.quantize_mx(codes[:].bitcast(fmt), scales[:], grouped[:])
            return [(codes[:, P * a : P * (a + 1)], scales[:, P * a : P * (a + 1)]) for a in range(tiles)]

        def g_values(h, picked, bank, tag):
            for u in range(2):
                rounded = keep.tile([P, HALF], BF16, name="rounded_g", tag="%s%d" % (tag, u), align_bytes=64)
                nc.vector.scalar_tensor_tensor(
                    rounded[:].rearrange("p (b s) -> p b s", s=16),
                    picked[:, u],
                    cp_t[:, h : h + 1],
                    rb_all[:, HALF * u : HALF * (u + 1)].rearrange("p (b s) -> p b s", s=16),
                    ALU.min,
                    ALU.mult,
                )
                turn_pairs(rounded, bank[:, u, :])

        def u_values(t, picked, bank):
            excess = []
            for u in range(2):
                excess.append(keep.tile([P, HALF], F32, name="excess", tag="excess%d" % u, align_bytes=64))
                nc.vector.tensor_scalar(
                    excess[u][:].rearrange("p (b s) -> p b s", s=16),
                    picked[:, u],
                    lo_t[:, t : t + 1],
                    0.0,
                    ALU.subtract,
                    ALU.max,
                )
            for u in range(2):
                rounded = work.tile([P, HALF], BF16, name="rounded", bufs=4, align_bytes=64)
                nc.vector.scalar_tensor_tensor(
                    rounded[:],
                    excess[u][:],
                    fk_t[:, t : t + 1],
                    ra_all[:, HALF * u : HALF * (u + 1)],
                    ALU.mult,
                    ALU.mult,
                )
                turn_pairs(rounded, bank[:, u, :])

        def moment(bank, t, u_op, g_op):
            nc.tensor.matmul_mx(
                bank[:, t, :],
                lhsT=u_op[0].bitcast(E4M3),
                lhsT_scale=u_op[1],
                rhs=g_op[0].bitcast(E5M2),
                rhs_scale=g_op[1],
                start=True,
                stop=True,
            )

        def directions(h, w_bank, v_banks):
            w_grouped = keep.tile([P, P, 4], BF16, name="w_grouped%d" % h, align_bytes=64)
            w_view = w_bank[:].rearrange("p t n -> p n t")
            nc.scalar.copy(w_grouped[:], w_view)
            codes = keep.tile([P, P], U32, name="w_codes%d" % h, align_bytes=64)
            scales = keep.tile([P, P], U8, name="w_scales%d" % h, align_bytes=64)
            nc.vector.quantize_mx(
                codes[:].bitcast(E5M2), scales[:], w_grouped[:].rearrange("p n t -> p (n t)")
            )
            for half in range(2):
                nc.tensor.matmul_mx(
                    v_banks[half][:],
                    lhsT=d_words[:, 2 * P * half : 2 * P * (half + 1)].bitcast(E2M1),
                    lhsT_scale=d_scales[:, P * half : P * (half + 1)],
                    rhs=codes[:].bitcast(E5M2),
                    rhs_scale=scales[:],
                    start=(h == 0),
                    stop=(h == 1),
                )

        rb_all = spread(rb_t, "rb_all")
        ra_all = spread(ra_t, "ra_all")
        w_banks = [psum.tile([P, 4, P], F32, name="w_bank%d" % h) for h in range(2)]

        g0_bank = psum.tile([P, 1, 2, P], F32, name="g0_bank")
        u01_bank = psum.tile([P, 2, 2, P], F32, name="u01_bank")
        u3_bank = psum.tile([P, 1, 2, P], F32, name="u3_bank")
        g1_bank = psum.tile([P, 1, 2, P], F32, name="g1_bank", tag="v_bank1")

        g_values(0, gather(g_tab[0], list_g, VECTOR_SHARE_G0, "chain_a"), g0_bank[:, 0], "rounded_g0")
        u_values(0, gather(x_tab[0], list_x, VECTOR_SHARE_X0, "chain_b"), u01_bank[:, 0])
        (g0,) = quantize(g0_bank, 1, E5M2, "g0", nc.vector.tensor_copy, "g0_grouped", "g0_codes")
        u2_bank = psum.tile([P, 1, 2, P], F32, name="u2_bank", tag="g0_bank")
        u_values(1, gather(x_tab[1], list_x, 0, "chain_a"), u01_bank[:, 1])
        u_values(2, gather(x_tab[2], list_x, 0, "chain_b"), u2_bank[:, 0])
        u_values(3, gather(x_tab[3], list_x, 0, "chain_a"), u3_bank[:, 0])
        g_values(1, gather(g_tab[1], list_g, 0, "chain_b"), g1_bank[:, 0], "excess")
        u_ops = quantize(u01_bank, 2, E4M3, "u01", nc.scalar.copy, "g_tab1", "chain_b")
        u_ops = u_ops + quantize(u2_bank, 1, E4M3, "u2", nc.scalar.copy, "u2_grouped", "cp_t")
        u_ops = u_ops + quantize(u3_bank, 1, E4M3, "u3", nc.scalar.copy, "u3_grouped", "u3_codes")
        (g1,) = quantize(g1_bank, 1, E5M2, "g1", nc.scalar.copy, "g1_grouped", "g1_codes")
        for t in range(4):
            moment(w_banks[0], t, u_ops[t], g0)
        for t in range(4):
            moment(w_banks[1], t, u_ops[t], g1)
        v_banks = [
            psum.tile([P, P], F32, name="v_bank0", tag="ra_all"),
            psum.tile([P, P], F32, name="v_bank1"),
        ]
        directions(0, w_banks[0], v_banks)
        directions(1, w_banks[1], v_banks)

        factor = keep.tile([P, 2, 1], F32, name="factor")
        nc.gpsimd.tensor_scalar(factor[:], gr_t[:], 0.02, 0.0, ALU.mult, ALU.add)
        even = keep.tile([P, 2, Q], F32, name="even")
        result = keep.tile([P, 2, Q], F32, name="result")
        for half in range(2):
            pairs = v_banks[half][:].rearrange("p (q e) -> p e q", e=2)
            nc.scalar.activation(even[:, half, :], pairs[:, 0], COPY, scale=factor[:, half, :])
            nc.vector.scalar_tensor_tensor(
                result[:, half, :], pairs[:, 1], factor[:, half, :], even[:, half, :], ALU.mult, ALU.add
            )
        nc.sync.dma_start(out.rearrange("(h p) q -> p h q", h=2), result[:])
